import numpy as np
import ml_dtypes


def mxq(x, axis, fmt="e4m3"):
    dtype, down = {"e4m3": (ml_dtypes.float8_e4m3fn, 7), "e5m2": (ml_dtypes.float8_e5m2, 14)}[fmt]
    v = np.moveaxis(np.asarray(x, np.float32).astype(ml_dtypes.bfloat16).astype(np.float64), axis, -1)
    blocks = v.reshape(v.shape[:-1] + (-1, 32))
    amax = np.abs(blocks).max(-1, keepdims=True)
    byte = np.maximum(np.where(amax > 0, np.frexp(amax)[1] - 1 + 127, 0) - down, 1)
    scale = np.exp2(byte - 127.0)
    codes = (blocks / scale).astype(np.float32).astype(dtype).astype(np.float64)
    return np.moveaxis((codes * scale).reshape(v.shape), -1, axis)


WIDE = False


def mx_kscale(k):
    if not WIDE:
        return np.ones(k)
    levels = np.array([10, -10, 5, -5, 0])
    if k % 512:
        return np.exp2(np.random.permutation(np.resize(levels, k // 32))).repeat(32)
    a = np.empty((k // 512, 16))
    for p in range(k // 512):
        a[p, :8] = np.random.permutation(np.resize(levels, 8))
        for g in range(8):
            far = levels[np.abs(levels - a[p, g]) >= 10]
            a[p, g + 8] = far[np.random.randint(len(far))]
    return np.exp2(a.ravel()).repeat(32)


def f64(x):
    return np.asarray(x).astype(np.float64)


def striped(idx):
    return np.tile(idx.reshape(-1, 16).T, (8, 1)).astype(np.uint16)


def unstriped(offs):
    return offs[:16].T.reshape(-1).astype(np.int64)


E2M1 = np.array([0.0, 0.5, 1.0, 1.5, 2.0, 3.0, 4.0, 6.0, -0.0, -0.5, -1.0, -1.5, -2.0, -3.0, -4.0, -6.0])


def pack_weight(w, fmt):
    k, n = w.shape
    w = f64(np.asarray(w, np.float32).astype(ml_dtypes.bfloat16)).reshape(k // 32, 32, n)
    amax = np.abs(w).max(1)
    if fmt == "e4m3":
        byte = np.frexp(amax)[1] - 1 + 127 - 7
    else:
        mant, ex = np.frexp(amax / 6.0)
        byte = np.where(mant > 0.5, ex, ex - 1) + 127
    byte = np.clip(np.where(amax > 0, byte, 1), 1, 254)
    scaled = (w * np.exp2(127.0 - byte)[:, None, :]).reshape(k, n).astype(np.float32)
    by_word = np.ascontiguousarray(scaled.reshape(k // 512, 128, 4, n).transpose(0, 1, 3, 2))
    if fmt == "e4m3":
        words = by_word.astype(ml_dtypes.float8_e4m3fn).view(np.uint8)
    else:
        c = by_word.astype(ml_dtypes.float4_e2m1fn).view(np.uint8) & 0xF
        words = (c[..., 0::2] | (c[..., 1::2] << 4)).reshape(k // 512, 128, 2 * n)
    return np.ascontiguousarray(words), np.ascontiguousarray(byte.astype(np.uint8).reshape(k // 512, 16, n))


def unpack_weight(words, scales, fmt):
    g, _, n = scales.shape
    words = np.ascontiguousarray(words).reshape(g, 128, n, -1)
    if fmt == "e4m3":
        vals = words.view(ml_dtypes.float8_e4m3fn).astype(np.float64)
    else:
        nib = np.empty((g, 128, n, 4), np.uint8)
        nib[..., 0::2] = words & 0xF
        nib[..., 1::2] = words >> 4
        vals = E2M1[nib]
    vals = vals * np.repeat(np.exp2(scales.astype(np.float64) - 127.0), 8, axis=1)[..., None]
    return vals.transpose(0, 1, 3, 2).reshape(g * 512, n)


def gelu(v):
    return 0.5 * v * (1.0 + np.tanh(np.sqrt(2.0 / np.pi) * (v + 0.044715 * v**3)))


def twice(P):
    return np.random.permutation(np.repeat(np.arange(P), 2))


K, H, T, S, P = 1024, 1024, 2048, 1024, 512


def setup_inputs():
    n = np.random.standard_normal
    s = mx_kscale(K)[:, None]
    u = mx_kscale(H)[:, None]
    d = {}
    d["tab_words"], d["tab_scales"] = pack_weight(n((K, T)) * s, "e4m3")
    d["offs"] = striped(np.random.permutation(T)[:S])
    d["pos1"] = striped(np.random.permutation(S)[:P])
    d["pos2"] = striped(np.random.permutation(S)[:P])
    d["pos3"] = striped(twice(P))
    common = n((K, H))
    d["w1"] = (2.8 * common / K ** 0.5 / s * u.T).astype(np.float32)
    d["w2"] = ((1.5 * common + 0.25 * n((K, H))) / K ** 0.5 / s).astype(np.float32)
    d["w4_words"], d["w4_scales"] = pack_weight(0.5 * n((H, H)) / H ** 0.5 / u, "e2m1")
    d["phase"] = (np.random.uniform(0.7, 1.1, H) / u[:, 0]).astype(np.float32)
    return d


def reference(tab_words, tab_scales, offs, pos1, pos2, pos3, w1, w2, w4_words, w4_scales, phase):
    v = unpack_weight(tab_words, tab_scales, "e4m3")[:, unstriped(offs)]
    drive = mxq(f64(w1), 0, "e4m3").T @ v
    load = mxq(f64(w2), 0, "e4m3").T @ v
    h = drive / (1.0 + np.abs(load))
    pair = h[:, unstriped(pos1)] + h[:, unstriped(pos2)]
    w4 = unpack_weight(w4_words, w4_scales, "e2m1")
    y = w4.T @ mxq(pair, 0, "e4m3")
    raised = y[:, unstriped(pos3)]
    out = raised - np.sin(f64(phase)[:, None] * h)
    return out

@@ -1,0 +1,242 @@
+from contextlib import ExitStack
+
+import concourse.mybir as mybir
+
+F32 = mybir.dt.float32
+BF16 = mybir.dt.bfloat16
+I32 = mybir.dt.int32
+U32 = mybir.dt.uint32
+U16 = mybir.dt.uint16
+U8 = mybir.dt.uint8
+FP8X4 = mybir.dt.float8_e4m3fn_x4
+FP4X4 = mybir.dt.float4_e2m1fn_x4
+ACT = mybir.ActivationFunctionType
+ALU = mybir.AluOpType
+
+K, H, T, S, PAIRS = 1024, 1024, 2048, 1024, 512
+P = 128
+PACK = 4
+PASS = P * PACK
+BANK = 512
+Y_WINDOW = 1040
+Y_TILES = 3
+FLOPS = 2 * (2 * K * H * S + H * H * PAIRS)
+ON_VECTOR = [(0, 1), (0, 2), (0, 3)]
+
+
+def tile_list_tissue_bubble_scores_kernel(
+    tc, tab_words, tab_scales, offs, pos1, pos2, pos3, w1, w2, w4_words, w4_scales, phase, out
+):
+    nc = tc.nc
+    with ExitStack() as ctx:
+        lists = ctx.enter_context(tc.tile_pool(name="lists", bufs=1))
+        keep = ctx.enter_context(tc.tile_pool(name="keep", bufs=1))
+        big = ctx.enter_context(tc.tile_pool(name="big", bufs=8))
+        ring2 = ctx.enter_context(tc.tile_pool(name="ring2", bufs=2))
+        ring3 = ctx.enter_context(tc.tile_pool(name="ring3", bufs=3))
+        psum = ctx.enter_context(tc.psum_pool(name="psum", bufs=4))
+
+        offs_sb = lists.tile([P, S // 16], U16, name="offs_sb")
+        pos1_sb = lists.tile([P, PAIRS // 16], U16, name="pos1_sb")
+        pos2_sb = lists.tile([P, PAIRS // 16], U16, name="pos2_sb")
+        pos3_sb = lists.tile([P, S // 16], U16, name="pos3_sb")
+
+        tab_sc = keep.tile([P, T], U8, name="tab_sc")
+        nc.vector.memset(tab_sc[:].bitcast(I32), 0)
+        w4_sc = keep.tile([P, 2, H], U8, name="w4_sc")
+        nc.vector.memset(w4_sc[:].bitcast(I32), 0)
+        y_win = [keep.tile([P, Y_WINDOW], F32, name="y_win%d" % i) for i in range(Y_TILES)]
+        for y in y_win:
+            nc.gpsimd.memset(y[:, PAIRS:], 0.0)
+
+        nc.sync.dma_start(offs_sb[:], offs)
+        tab = [keep.tile([P, T], I32, name="tab%d" % a) for a in range(2)]
+
+        def load_tab(a):
+            nc.sync.dma_start(out=tab[a][:], in_=tab_words[a].rearrange("p t i -> p (t i)").bitcast(I32))
+
+        raw = {}
+
+        def load_w(b, c):
+            w = (w2, w1)[c // 2]
+            a = c % 2
+            raw[b, c] = big.tile([P, PACK, PASS], F32, name="big", tag="big")
+            nc.sync.dma_start(
+                out=raw[b, c][:],
+                in_=w[a * PASS : (a + 1) * PASS, b * PASS : (b + 1) * PASS].rearrange("(p j) c -> p j c", j=PACK),
+            )
+
+        load_tab(0)
+        for q in range(4):
+            nc.sync.dma_start(
+                out=tab_sc[32 * q : 32 * q + 8, :].bitcast(I32),
+                in_=tab_scales[:, 4 * q : 4 * q + 4, :].bitcast(I32),
+            )
+        load_w(0, 0)
+        load_tab(1)
+        for c in range(1, 4):
+            load_w(0, c)
+        nc.sync.dma_start(pos1_sb[:], pos1)
+        nc.sync.dma_start(pos2_sb[:], pos2)
+        for c in range(4):
+            load_w(1, c)
+        w4_raw = keep.tile([P, 2, 2 * H // 4], I32, name="w4_raw")
+        nc.sync.dma_start(out=w4_raw[:], in_=w4_words.rearrange("a p c -> p a c").bitcast(I32))
+        for q in range(4):
+            nc.sync.dma_start(
+                out=w4_sc[32 * q : 32 * q + 4, :, :].bitcast(I32),
+                in_=w4_scales[:, 4 * q : 4 * q + 4, :].rearrange("a r n -> r a n").bitcast(I32),
+            )
+        nc.sync.dma_start(pos3_sb[:], pos3)
+        phase_sb = keep.tile([P, 2, PACK], F32, name="phase_sb")
+        nc.sync.dma_start(out=phase_sb[:], in_=phase.rearrange("(b p t) -> p b t", b=2, t=PACK))
+
+        warm = keep.tile([P, 2], F32, name="warm")
+        nc.gpsimd.memset(warm[:], 1.0)
+        nc.scalar.activation(out=warm[:, 1:2], in_=warm[:, 0:1], func=ACT.Abs_reciprocal_sqrt)
+
+        v_words = [keep.tile([P, S], U32, name="v_words%d" % a, align_bytes=64) for a in range(2)]
+        v_sc = keep.tile([P, S], U8, name="v_sc", align_bytes=64)
+
+        def gather_tab(a):
+            nc.vector.tensor_copy(v_words[a][:], tab[a][:].bitcast(U32).indirect(offs_sb[:]))
+
+        codes = {}
+        scales = {}
+
+        def quantize_w(b, c):
+            grouped = ring3.tile([P, PACK, P, PACK], BF16, name="grouped", tag="grouped", align_bytes=64)
+            dst = grouped[:].rearrange("p (u v) m j -> p m u j v", v=2)
+            src = raw[b, c][:].rearrange("p j (m u v) -> p m u j v", u=2, v=2)
+            if (b, c) in ON_VECTOR:
+                nc.vector.tensor_copy(out=dst, in_=src)
+            else:
+                nc.scalar.copy(out=dst, in_=src)
+            codes[b, c] = keep.tile([P, PASS], U32, name="codes%d%d" % (b, c), align_bytes=64)
+            scales[b, c] = keep.tile([P, PASS], U8, name="scales%d%d" % (b, c), align_bytes=64)
+            nc.vector.quantize_mx(
+                out=codes[b, c][:].bitcast(FP8X4),
+                scales=scales[b, c][:],
+                in_=grouped[:].rearrange("p t m j -> p (t m j)"),
+            )
+
+        def first_product(acc, b, which, t, half):
+            cols = slice(t * P, (t + 1) * P)
+            js = slice(half * BANK, (half + 1) * BANK)
+            for a in range(2):
+                c = 2 * which + a
+                nc.tensor.matmul_mx(
+                    out=acc[:],
+                    lhsT=codes[b, c][:, cols].bitcast(FP8X4),
+                    lhsT_scale=scales[b, c][:, cols],
+                    rhs=v_words[a][:, js].bitcast(FP8X4),
+                    rhs_scale=v_sc[4 * a :, js],
+                    start=(a == 0),
+                    stop=(a == 1),
+                )
+
+        recip = {}
+
+        def denominators(b, t):
+            mag = ring2.tile([P, S], F32, name="mag", tag="mag")
+            for half in range(2):
+                acc = psum.tile([P, BANK], F32, name="load", tag="load")
+                first_product(acc, b, 0, t, half)
+                nc.scalar.activation(out=mag[:, half * BANK : (half + 1) * BANK], in_=acc[:], func=ACT.Abs)
+            r = ring3.tile([P, S], F32, name="recip", tag="recip")
+            nc.scalar.activation(out=r[:], in_=mag[:], func=ACT.Abs_reciprocal_sqrt, bias=1.0)
+            nc.scalar.activation(out=r[:], in_=r[:], func=ACT.Square)
+            recip[b, t] = r
+
+        h = {}
+
+        def features(b, t, pair):
+            h[b, t] = keep.tile([P, S], F32, name="h%d%d" % (b, t))
+            for half in range(2):
+                js = slice(half * BANK, (half + 1) * BANK)
+                acc = psum.tile([P, BANK], F32, name="drive", tag="drive")
+                first_product(acc, b, 1, t, half)
+                nc.vector.tensor_tensor(out=h[b, t][:, js], in0=acc[:], in1=recip[b, t][:, js], op=ALU.mult)
+            first = ring2.tile([P, PAIRS], F32, name="first", tag="first")
+            nc.vector.tensor_copy(first[:], h[b, t][:].indirect(pos1_sb[:]))
+            nc.vector.tensor_tensor(pair[:, t, :], h[b, t][:].indirect(pos2_sb[:]), first[:], ALU.add)
+
+        pair_codes = []
+        pair_scales = []
+
+        def quantize_pair(b, pair):
+            grouped = ring3.tile([P, PAIRS, PACK], BF16, name="grouped", tag="grouped", align_bytes=64)
+            nc.vector.tensor_copy(
+                out=grouped[:].rearrange("p (c i) t -> p c t i", i=4),
+                in_=pair[:].rearrange("p t (c i) -> p c t i", i=4),
+            )
+            pc = keep.tile([P, PAIRS], U32, name="pair_codes%d" % b, align_bytes=64)
+            ps = keep.tile([P, PAIRS], U8, name="pair_scales%d" % b, align_bytes=64)
+            nc.vector.quantize_mx(
+                out=pc[:].bitcast(FP8X4), scales=ps[:], in_=grouped[:].rearrange("p m t -> p (m t)")
+            )
+            pair_codes.append(pc)
+            pair_scales.append(ps)
+
+        gather_tab(0)
+        nc.vector.tensor_copy(v_sc[:], tab_sc[:].indirect(offs_sb[:]))
+        quantize_w(0, 0)
+        gather_tab(1)
+        for c in range(1, 4):
+            quantize_w(0, c)
+
+        w4_dealt = keep.tile([P, 2 * 2 * H], U8, name="w4_dealt", align_bytes=64)
+        w4_sc_dealt = keep.tile([P, 2 * H], U8, name="w4_sc_dealt", align_bytes=64)
+
+        denominators(0, 0)
+        for b in range(2):
+            pair = ring2.tile([P, PACK, PAIRS], F32, name="pair", tag="pair")
+            for t in range(PACK):
+                nxt = b * PACK + t + 1
+                if nxt < 2 * PACK and (b, t) != (0, PACK - 1):
+                    denominators(nxt // PACK, nxt % PACK)
+                if b == 0:
+                    quantize_w(1, t)
+                if (b, t) == (0, PACK - 1):
+                    denominators(1, 0)
+                features(b, t, pair)
+            quantize_pair(b, pair)
+            if b == 0:
+                nc.vector.tensor_copy(
+                    out=w4_dealt[:].bitcast(U16).rearrange("p (g t q) -> p g t q", g=4, t=PACK),
+                    in_=w4_raw[:].rearrange("p a c -> p (a c)").bitcast(U16).rearrange("p (g q t) -> p g t q", g=4, t=PACK),
+                )
+                nc.vector.tensor_copy(
+                    out=w4_sc_dealt[:].rearrange("p (g t q) -> p g t q", g=4, t=PACK),
+                    in_=w4_sc[:].rearrange("p a (b q t) -> p (a b) t q", b=2, t=PACK),
+                )
+
+        neg_phase = {}
+        for b in (1, 0):
+            neg_phase[b] = ring2.tile([P, PACK], F32, name="neg_phase", tag="mag")
+            nc.scalar.activation(out=neg_phase[b][:], in_=phase_sb[:, b, :], func=ACT.Copy, scale=-1.0)
+
+        out_rows = out.rearrange("(b p t) j -> b t p j", b=2, t=PACK)
+        for b in range(2):
+            for t in range(PACK):
+                s = b * PACK + t
+                work = big.tile([P, 2, S], F32, name="work", tag="big")
+                nc.scalar.activation(
+                    out=work[:, 0, :], in_=h[b, t][:], func=ACT.Sin, scale=neg_phase[b][:, t : t + 1]
+                )
+                acc = psum.tile([P, BANK], F32, name="y", tag="load")
+                for a in range(2):
+                    c0 = a * H + s * P
+                    nc.tensor.matmul_mx(
+                        out=acc[:],
+                        lhsT=w4_dealt[:, 2 * c0 : 2 * (c0 + P)].bitcast(FP4X4),
+                        lhsT_scale=w4_sc_dealt[:, c0 : c0 + P],
+                        rhs=pair_codes[a][:].bitcast(FP8X4),
+                        rhs_scale=pair_scales[a][:],
+                        start=(a == 0),
+                        stop=(a == 1),
+                    )
+                y = y_win[s % Y_TILES]
+                nc.scalar.copy(out=y[:, :PAIRS], in_=acc[:])
+                nc.vector.tensor_tensor(work[:, 1, :], y[:].indirect(pos3_sb[:]), work[:, 0, :], ALU.add)
+                nc.sync.dma_start(out=out_rows[b, t], in_=work[:, 1, :])

@@ -18,10 +18,12 @@ P = 128
 PACK = 4
 PASS = P * PACK
 BANK = 512
+SLICES = H // P
 Y_WINDOW = 1040
 Y_TILES = 3
 FLOPS = 2 * (2 * K * H * S + H * H * PAIRS)
-ON_VECTOR = [(0, 1), (0, 2), (0, 3)]
+CAST_BY = [["VS", "VS", "V", "V"], ["V", "V", "S", "S"]]
+SPLIT_QUANTIZE = [(0, 1)]
 
 
 def tile_list_tissue_bubble_scores_kernel(
@@ -32,7 +34,6 @@ def tile_list_tissue_bubble_scores_kernel(
         lists = ctx.enter_context(tc.tile_pool(name="lists", bufs=1))
         keep = ctx.enter_context(tc.tile_pool(name="keep", bufs=1))
         big = ctx.enter_context(tc.tile_pool(name="big", bufs=8))
-        ring2 = ctx.enter_context(tc.tile_pool(name="ring2", bufs=2))
         ring3 = ctx.enter_context(tc.tile_pool(name="ring3", bufs=3))
         psum = ctx.enter_context(tc.psum_pool(name="psum", bufs=4))
 
@@ -42,9 +43,9 @@ def tile_list_tissue_bubble_scores_kernel(
         pos3_sb = lists.tile([P, S // 16], U16, name="pos3_sb")
 
         tab_sc = keep.tile([P, T], U8, name="tab_sc")
-        nc.vector.memset(tab_sc[:].bitcast(I32), 0)
+        nc.gpsimd.memset(tab_sc[:].bitcast(I32), 0)
         w4_sc = keep.tile([P, 2, H], U8, name="w4_sc")
-        nc.vector.memset(w4_sc[:].bitcast(I32), 0)
+        nc.gpsimd.memset(w4_sc[:].bitcast(I32), 0)
         y_win = [keep.tile([P, Y_WINDOW], F32, name="y_win%d" % i) for i in range(Y_TILES)]
         for y in y_win:
             nc.gpsimd.memset(y[:, PAIRS:], 0.0)
@@ -66,29 +67,37 @@ def tile_list_tissue_bubble_scores_kernel(
                 in_=w[a * PASS : (a + 1) * PASS, b * PASS : (b + 1) * PASS].rearrange("(p j) c -> p j c", j=PACK),
             )
 
-        load_tab(0)
-        for q in range(4):
-            nc.sync.dma_start(
-                out=tab_sc[32 * q : 32 * q + 8, :].bitcast(I32),
-                in_=tab_scales[:, 4 * q : 4 * q + 4, :].bitcast(I32),
-            )
-        load_w(0, 0)
-        load_tab(1)
-        for c in range(1, 4):
-            load_w(0, c)
+        def load_tab_scales():
+            for q in range(4):
+                nc.sync.dma_start(
+                    out=tab_sc[32 * q : 32 * q + 8, :].bitcast(I32),
+                    in_=tab_scales[:, 4 * q : 4 * q + 4, :].bitcast(I32),
+                )
+
+        w4_raw = keep.tile([P, 2, 2 * H // 4], I32, name="w4_raw")
+
+        def load_w4():
+            for q in range(4):
+                nc.sync.dma_start(
+                    out=w4_sc[32 * q : 32 * q + 4, :, :].bitcast(I32),
+                    in_=w4_scales[:, 4 * q : 4 * q + 4, :].rearrange("a r n -> r a n").bitcast(I32),
+                )
+            nc.sync.dma_start(out=w4_raw[:], in_=w4_words.rearrange("a p c -> p a c").bitcast(I32))
+
+        phase_sb = keep.tile([P, 2, PACK], F32, name="phase_sb")
         nc.sync.dma_start(pos1_sb[:], pos1)
         nc.sync.dma_start(pos2_sb[:], pos2)
+        load_tab_scales()
+        load_tab(0)
+        load_tab(1)
+        load_w(0, 0)
+        load_w(0, 1)
+        load_w(0, 2)
+        load_w(0, 3)
         for c in range(4):
             load_w(1, c)
-        w4_raw = keep.tile([P, 2, 2 * H // 4], I32, name="w4_raw")
-        nc.sync.dma_start(out=w4_raw[:], in_=w4_words.rearrange("a p c -> p a c").bitcast(I32))
-        for q in range(4):
-            nc.sync.dma_start(
-                out=w4_sc[32 * q : 32 * q + 4, :, :].bitcast(I32),
-                in_=w4_scales[:, 4 * q : 4 * q + 4, :].rearrange("a r n -> r a n").bitcast(I32),
-            )
+        load_w4()
         nc.sync.dma_start(pos3_sb[:], pos3)
-        phase_sb = keep.tile([P, 2, PACK], F32, name="phase_sb")
         nc.sync.dma_start(out=phase_sb[:], in_=phase.rearrange("(b p t) -> p b t", b=2, t=PACK))
 
         warm = keep.tile([P, 2], F32, name="warm")
@@ -108,17 +117,22 @@ def tile_list_tissue_bubble_scores_kernel(
             grouped = ring3.tile([P, PACK, P, PACK], BF16, name="grouped", tag="grouped", align_bytes=64)
             dst = grouped[:].rearrange("p (u v) m j -> p m u j v", v=2)
             src = raw[b, c][:].rearrange("p j (m u v) -> p m u j v", u=2, v=2)
-            if (b, c) in ON_VECTOR:
-                nc.vector.tensor_copy(out=dst, in_=src)
-            else:
-                nc.scalar.copy(out=dst, in_=src)
+            engines = CAST_BY[b][c]
+            for i, engine in enumerate(engines):
+                copy = nc.vector.tensor_copy if engine == "V" else nc.scalar.copy
+                if len(engines) == 1:
+                    copy(out=dst, in_=src)
+                else:
+                    copy(out=dst[:, :, i], in_=src[:, :, i])
             codes[b, c] = keep.tile([P, PASS], U32, name="codes%d%d" % (b, c), align_bytes=64)
             scales[b, c] = keep.tile([P, PASS], U8, name="scales%d%d" % (b, c), align_bytes=64)
-            nc.vector.quantize_mx(
-                out=codes[b, c][:].bitcast(FP8X4),
-                scales=scales[b, c][:],
-                in_=grouped[:].rearrange("p t m j -> p (t m j)"),
-            )
+            width = PASS // 2 if (b, c) in SPLIT_QUANTIZE else PASS
+            for c0 in range(0, PASS, width):
+                nc.vector.quantize_mx(
+                    out=codes[b, c][:, c0 : c0 + width].bitcast(FP8X4),
+                    scales=scales[b, c][:, c0 : c0 + width],
+                    in_=grouped[:].rearrange("p t m j -> p (t m j)")[:, PACK * c0 : PACK * (c0 + width)],
+                )
 
         def first_product(acc, b, which, t, half):
             cols = slice(t * P, (t + 1) * P)
@@ -135,102 +149,133 @@ def tile_list_tissue_bubble_scores_kernel(
                     stop=(a == 1),
                 )
 
+        root = {}
         recip = {}
 
-        def denominators(b, t):
-            mag = ring2.tile([P, S], F32, name="mag", tag="mag")
+        def denominators(s):
+            b, t = divmod(s, PACK)
+            root[s] = ring3.tile([P, S], F32, name="root", tag="root", align_bytes=64)
             for half in range(2):
                 acc = psum.tile([P, BANK], F32, name="load", tag="load")
                 first_product(acc, b, 0, t, half)
-                nc.scalar.activation(out=mag[:, half * BANK : (half + 1) * BANK], in_=acc[:], func=ACT.Abs)
-            r = ring3.tile([P, S], F32, name="recip", tag="recip")
-            nc.scalar.activation(out=r[:], in_=mag[:], func=ACT.Abs_reciprocal_sqrt, bias=1.0)
-            nc.scalar.activation(out=r[:], in_=r[:], func=ACT.Square)
-            recip[b, t] = r
+                nc.scalar.activation(out=root[s][:, half * BANK : (half + 1) * BANK], in_=acc[:], func=ACT.Abs)
+            nc.scalar.activation(out=root[s][:], in_=root[s][:], func=ACT.Abs_reciprocal_sqrt, bias=1.0)
+            recip[s] = ring3.tile([P, S], F32, name="recip", tag="recip")
+            nc.scalar.activation(out=recip[s][:], in_=root[s][:], func=ACT.Square)
 
-        h = {}
+        h = [keep.tile([P, S], F32, name="h%d" % s) for s in range(SLICES)]
+        pair = [keep.tile([P, PACK, PAIRS], F32, name="pair%d" % b, align_bytes=64) for b in range(2)]
 
-        def features(b, t, pair):
-            h[b, t] = keep.tile([P, S], F32, name="h%d%d" % (b, t))
-            for half in range(2):
-                js = slice(half * BANK, (half + 1) * BANK)
-                acc = psum.tile([P, BANK], F32, name="drive", tag="drive")
-                first_product(acc, b, 1, t, half)
-                nc.vector.tensor_tensor(out=h[b, t][:, js], in0=acc[:], in1=recip[b, t][:, js], op=ALU.mult)
-            first = ring2.tile([P, PAIRS], F32, name="first", tag="first")
-            nc.vector.tensor_copy(first[:], h[b, t][:].indirect(pos1_sb[:]))
-            nc.vector.tensor_tensor(pair[:, t, :], h[b, t][:].indirect(pos2_sb[:]), first[:], ALU.add)
+        def features(s, half):
+            b, t = divmod(s, PACK)
+            js = slice(half * BANK, (half + 1) * BANK)
+            acc = psum.tile([P, BANK], F32, name="drive", tag="drive")
+            first_product(acc, b, 1, t, half)
+            nc.vector.tensor_tensor(out=h[s][:, js], in0=acc[:], in1=recip[s][:, js], op=ALU.mult)
 
-        pair_codes = []
-        pair_scales = []
+        def first_stop(s, held, m0, m1):
+            nc.vector.tensor_copy(held[:, m0:m1], h[s][:].indirect(pos1_sb[:, m0 // 16 : m1 // 16]))
 
-        def quantize_pair(b, pair):
-            grouped = ring3.tile([P, PAIRS, PACK], BF16, name="grouped", tag="grouped", align_bytes=64)
-            nc.vector.tensor_copy(
-                out=grouped[:].rearrange("p (c i) t -> p c t i", i=4),
-                in_=pair[:].rearrange("p t (c i) -> p c t i", i=4),
+        def second_stop(s, held, m0, m1):
+            b, t = divmod(s, PACK)
+            nc.vector.tensor_tensor(
+                pair[b][:, t, m0:m1], h[s][:].indirect(pos2_sb[:, m0 // 16 : m1 // 16]), held[:, m0:m1], ALU.add
             )
-            pc = keep.tile([P, PAIRS], U32, name="pair_codes%d" % b, align_bytes=64)
-            ps = keep.tile([P, PAIRS], U8, name="pair_scales%d" % b, align_bytes=64)
+
+        pair_codes = [keep.tile([P, PAIRS], U32, name="pair_codes%d" % b, align_bytes=64) for b in range(2)]
+        pair_scales = [keep.tile([P, PAIRS], U8, name="pair_scales%d" % b, align_bytes=64) for b in range(2)]
+
+        def interleave_pair(b, grouped, copy, m0, m1):
+            copy(
+                out=grouped[:, PACK * m0 : PACK * m1].rearrange("p (c i t) -> p c t i", i=4, t=PACK),
+                in_=pair[b][:, :, m0:m1].rearrange("p t (c i) -> p c t i", i=4),
+            )
+
+        def quantize_pair(b, grouped, m0, m1):
             nc.vector.quantize_mx(
-                out=pc[:].bitcast(FP8X4), scales=ps[:], in_=grouped[:].rearrange("p m t -> p (m t)")
+                out=pair_codes[b][:, m0:m1].bitcast(FP8X4),
+                scales=pair_scales[b][:, m0:m1],
+                in_=grouped[:, PACK * m0 : PACK * m1],
             )
-            pair_codes.append(pc)
-            pair_scales.append(ps)
 
-        gather_tab(0)
+        w4_dealt = {}
+        w4_sc_dealt = {}
+
+        def deal_w4(b, words_tag, scales_tag):
+            w4_dealt[b] = keep.tile([P, 2, 2 * PASS], U8, name="w4_dealt%d" % b, tag=words_tag, align_bytes=64)
+            w4_sc_dealt[b] = keep.tile([P, 2, PASS], U8, name="w4_sc_dealt%d" % b, tag=scales_tag, align_bytes=64)
+            cols = slice(b * PASS, (b + 1) * PASS)
+            nc.vector.tensor_copy(
+                out=w4_dealt[b][:].bitcast(U16).rearrange("p a (t q) -> p a t q", t=PACK),
+                in_=w4_raw[:].bitcast(U16)[:, :, cols].rearrange("p a (q t) -> p a t q", t=PACK),
+            )
+            nc.vector.tensor_copy(
+                out=w4_sc_dealt[b][:].rearrange("p a (t q) -> p a t q", t=PACK),
+                in_=w4_sc[:, :, cols].rearrange("p a (q t) -> p a t q", t=PACK),
+            )
+
         nc.vector.tensor_copy(v_sc[:], tab_sc[:].indirect(offs_sb[:]))
-        quantize_w(0, 0)
+        gather_tab(0)
         gather_tab(1)
-        for c in range(1, 4):
+        for c in range(4):
             quantize_w(0, c)
 
-        w4_dealt = keep.tile([P, 2 * 2 * H], U8, name="w4_dealt", align_bytes=64)
-        w4_sc_dealt = keep.tile([P, 2 * H], U8, name="w4_sc_dealt", align_bytes=64)
+        last = SLICES - 1
+        denominators(0)
+        features(0, 0)
+        features(0, 1)
+        for s in range(last - 1):
+            if s < PACK:
+                quantize_w(1, s)
+            denominators(s + 1)
+            features(s + 1, 0)
+            first_stop(s, root[s + 1], 0, PAIRS)
+            features(s + 1, 1)
+            second_stop(s, root[s + 1], 0, PAIRS)
+        deal_w4(0, "w4_dealt0", "w4_sc_dealt0")
+        denominators(last)
+        features(last, 0)
+        features(last, 1)
+        held = [recip[last][:, :PAIRS], recip[last][:, PAIRS:]]
+        for i in range(2):
+            first_stop(last - 1 + i, held[i], 0, PAIRS)
+        for i in range(2):
+            second_stop(last - 1 + i, held[i], 0, PAIRS)
 
-        denominators(0, 0)
-        for b in range(2):
-            pair = ring2.tile([P, PACK, PAIRS], F32, name="pair", tag="pair")
-            for t in range(PACK):
-                nxt = b * PACK + t + 1
-                if nxt < 2 * PACK and (b, t) != (0, PACK - 1):
-                    denominators(nxt // PACK, nxt % PACK)
-                if b == 0:
-                    quantize_w(1, t)
-                if (b, t) == (0, PACK - 1):
-                    denominators(1, 0)
-                features(b, t, pair)
-            quantize_pair(b, pair)
-            if b == 0:
-                nc.vector.tensor_copy(
-                    out=w4_dealt[:].bitcast(U16).rearrange("p (g t q) -> p g t q", g=4, t=PACK),
-                    in_=w4_raw[:].rearrange("p a c -> p (a c)").bitcast(U16).rearrange("p (g q t) -> p g t q", g=4, t=PACK),
-                )
-                nc.vector.tensor_copy(
-                    out=w4_sc_dealt[:].rearrange("p (g t q) -> p g t q", g=4, t=PACK),
-                    in_=w4_sc[:].rearrange("p a (b q t) -> p (a b) t q", b=2, t=PACK),
-                )
+        grouped0 = root[last][:].bitcast(BF16)
+        interleave_pair(0, grouped0, nc.scalar.copy, 0, PAIRS)
+        quantize_pair(0, grouped0, 0, PAIRS)
+        grouped1 = keep.tile([P, PACK * PAIRS], BF16, name="grouped1", align_bytes=64)
+        halves = [(0, PAIRS // 2), (PAIRS // 2, PAIRS)]
 
-        neg_phase = {}
-        for b in (1, 0):
-            neg_phase[b] = ring2.tile([P, PACK], F32, name="neg_phase", tag="mag")
-            nc.scalar.activation(out=neg_phase[b][:], in_=phase_sb[:, b, :], func=ACT.Copy, scale=-1.0)
+        neg_phase = pair[0][:, 0, :SLICES]
+        nc.scalar.activation(
+            out=neg_phase, in_=phase_sb[:].rearrange("p b t -> p (b t)"), func=ACT.Copy, scale=-1.0
+        )
 
+        work = [big.tile([P, 2, S], F32, name="work", tag="big") for s in range(SLICES)]
+
+        def phase_score(s):
+            nc.scalar.activation(out=work[s][:, 0, :], in_=h[s][:], func=ACT.Sin, scale=neg_phase[:, s : s + 1])
+
+        phase_score(0)
+        interleave_pair(1, grouped1, nc.vector.tensor_copy, *halves[0])
+        interleave_pair(1, grouped1, nc.scalar.copy, *halves[1])
+        for m0, m1 in halves:
+            quantize_pair(1, grouped1, m0, m1)
+        deal_w4(1, "pair1", "grouped1")
         out_rows = out.rearrange("(b p t) j -> b t p j", b=2, t=PACK)
         for b in range(2):
             for t in range(PACK):
                 s = b * PACK + t
-                work = big.tile([P, 2, S], F32, name="work", tag="big")
-                nc.scalar.activation(
-                    out=work[:, 0, :], in_=h[b, t][:], func=ACT.Sin, scale=neg_phase[b][:, t : t + 1]
-                )
+                if s > 0:
+                    phase_score(s)
                 acc = psum.tile([P, BANK], F32, name="y", tag="load")
                 for a in range(2):
-                    c0 = a * H + s * P
                     nc.tensor.matmul_mx(
                         out=acc[:],
-                        lhsT=w4_dealt[:, 2 * c0 : 2 * (c0 + P)].bitcast(FP4X4),
-                        lhsT_scale=w4_sc_dealt[:, c0 : c0 + P],
+                        lhsT=w4_dealt[b][:, a, 2 * t * P : 2 * (t + 1) * P].bitcast(FP4X4),
+                        lhsT_scale=w4_sc_dealt[b][:, a, t * P : (t + 1) * P],
                         rhs=pair_codes[a][:].bitcast(FP8X4),
                         rhs_scale=pair_scales[a][:],
                         start=(a == 0),
@@ -238,5 +283,10 @@ def tile_list_tissue_bubble_scores_kernel(
                     )
                 y = y_win[s % Y_TILES]
                 nc.scalar.copy(out=y[:, :PAIRS], in_=acc[:])
-                nc.vector.tensor_tensor(work[:, 1, :], y[:].indirect(pos3_sb[:]), work[:, 0, :], ALU.add)
-                nc.sync.dma_start(out=out_rows[b, t], in_=work[:, 1, :])
+                cuts = [0, 512, 768, S] if s == last else [0, S]
+                for j0, j1 in zip(cuts, cuts[1:]):
+                    js = slice(j0, j1)
+                    nc.vector.tensor_tensor(
+                        work[s][:, 1, js], y[:].indirect(pos3_sb[:, j0 // 16 : j1 // 16]), work[s][:, 0, js], ALU.add
+                    )
+                    nc.sync.dma_start(out=out_rows[b, t][:, js], in_=work[s][:, 1, js])

@@ -22,7 +22,7 @@ SLICES = H // P
 Y_WINDOW = 1040
 Y_TILES = 3
 FLOPS = 2 * (2 * K * H * S + H * H * PAIRS)
-CAST_BY = [["VS", "VS", "V", "V"], ["V", "V", "S", "S"]]
+CAST_BY = [["VS", "VS", "V", "V"], ["V", "V", "VS", "S"]]
 SPLIT_QUANTIZE = [(0, 1)]
 
 
@@ -154,7 +154,7 @@ def tile_list_tissue_bubble_scores_kernel(
 
         def denominators(s):
             b, t = divmod(s, PACK)
-            root[s] = ring3.tile([P, S], F32, name="root", tag="root", align_bytes=64)
+            root[s] = ring3.tile([P, S], F32, name="root", tag="root", align_bytes=64, bufs=4)
             for half in range(2):
                 acc = psum.tile([P, BANK], F32, name="load", tag="load")
                 first_product(acc, b, 0, t, half)
@@ -169,7 +169,7 @@ def tile_list_tissue_bubble_scores_kernel(
         def features(s, half):
             b, t = divmod(s, PACK)
             js = slice(half * BANK, (half + 1) * BANK)
-            acc = psum.tile([P, BANK], F32, name="drive", tag="drive")
+            acc = psum.tile([P, BANK], F32, name="drive", tag="drive%d" % half, bufs=2)
             first_product(acc, b, 1, t, half)
             nc.vector.tensor_tensor(out=h[s][:, js], in0=acc[:], in1=recip[s][:, js], op=ALU.mult)
 
@@ -201,18 +201,20 @@ def tile_list_tissue_bubble_scores_kernel(
         w4_dealt = {}
         w4_sc_dealt = {}
 
-        def deal_w4(b, words_tag, scales_tag):
-            w4_dealt[b] = keep.tile([P, 2, 2 * PASS], U8, name="w4_dealt%d" % b, tag=words_tag, align_bytes=64)
-            w4_sc_dealt[b] = keep.tile([P, 2, PASS], U8, name="w4_sc_dealt%d" % b, tag=scales_tag, align_bytes=64)
-            cols = slice(b * PASS, (b + 1) * PASS)
+        def deal_w4(t0, t1, words_tag, scales_tag):
+            words = keep.tile([P, 4, t1 - t0, 2 * P], U8, name="w4_dealt%d" % t0, tag=words_tag, align_bytes=64)
+            planes = keep.tile([P, 4, t1 - t0, P], U8, name="w4_sc_dealt%d" % t0, tag=scales_tag, align_bytes=64)
             nc.vector.tensor_copy(
-                out=w4_dealt[b][:].bitcast(U16).rearrange("p a (t q) -> p a t q", t=PACK),
-                in_=w4_raw[:].bitcast(U16)[:, :, cols].rearrange("p a (q t) -> p a t q", t=PACK),
+                out=words[:].bitcast(U16),
+                in_=w4_raw[:].bitcast(U16).rearrange("p a (b q t) -> p (a b) t q", b=2, t=PACK)[:, :, t0:t1, :],
             )
             nc.vector.tensor_copy(
-                out=w4_sc_dealt[b][:].rearrange("p a (t q) -> p a t q", t=PACK),
-                in_=w4_sc[:, :, cols].rearrange("p a (q t) -> p a t q", t=PACK),
+                out=planes[:],
+                in_=w4_sc[:].rearrange("p a (b q t) -> p (a b) t q", b=2, t=PACK)[:, :, t0:t1, :],
             )
+            for t in range(t0, t1):
+                w4_dealt[t] = words[:, :, t - t0, :]
+                w4_sc_dealt[t] = planes[:, :, t - t0, :]
 
         nc.vector.tensor_copy(v_sc[:], tab_sc[:].indirect(offs_sb[:]))
         gather_tab(0)
@@ -232,7 +234,7 @@ def tile_list_tissue_bubble_scores_kernel(
             first_stop(s, root[s + 1], 0, PAIRS)
             features(s + 1, 1)
             second_stop(s, root[s + 1], 0, PAIRS)
-        deal_w4(0, "w4_dealt0", "w4_sc_dealt0")
+        deal_w4(0, 1, "w4_dealt0", "w4_sc_dealt0")
         denominators(last)
         features(last, 0)
         features(last, 1)
@@ -253,40 +255,43 @@ def tile_list_tissue_bubble_scores_kernel(
             out=neg_phase, in_=phase_sb[:].rearrange("p b t -> p (b t)"), func=ACT.Copy, scale=-1.0
         )
 
-        work = [big.tile([P, 2, S], F32, name="work", tag="big") for s in range(SLICES)]
+        score = {}
 
         def phase_score(s):
-            nc.scalar.activation(out=work[s][:, 0, :], in_=h[s][:], func=ACT.Sin, scale=neg_phase[:, s : s + 1])
+            score[s] = ring3.tile([P, S], F32, name="score", tag="recip")
+            nc.scalar.activation(out=score[s][:], in_=h[s][:], func=ACT.Sin, scale=neg_phase[:, s : s + 1])
 
         phase_score(0)
+        phase_score(PACK)
         interleave_pair(1, grouped1, nc.vector.tensor_copy, *halves[0])
         interleave_pair(1, grouped1, nc.scalar.copy, *halves[1])
         for m0, m1 in halves:
             quantize_pair(1, grouped1, m0, m1)
-        deal_w4(1, "pair1", "grouped1")
+        deal_w4(1, PACK, "pair1", "grouped1")
         out_rows = out.rearrange("(b p t) j -> b t p j", b=2, t=PACK)
-        for b in range(2):
-            for t in range(PACK):
+        for t in range(PACK):
+            for b in range(2):
                 s = b * PACK + t
-                if s > 0:
+                if t > 0:
                     phase_score(s)
-                acc = psum.tile([P, BANK], F32, name="y", tag="load")
+                acc = psum.tile([P, BANK], F32, name="y", tag="drive0", bufs=2)
                 for a in range(2):
                     nc.tensor.matmul_mx(
                         out=acc[:],
-                        lhsT=w4_dealt[b][:, a, 2 * t * P : 2 * (t + 1) * P].bitcast(FP4X4),
-                        lhsT_scale=w4_sc_dealt[b][:, a, t * P : (t + 1) * P],
+                        lhsT=w4_dealt[t][:, 2 * a + b, :].bitcast(FP4X4),
+                        lhsT_scale=w4_sc_dealt[t][:, 2 * a + b, :],
                         rhs=pair_codes[a][:].bitcast(FP8X4),
                         rhs_scale=pair_scales[a][:],
                         start=(a == 0),
                         stop=(a == 1),
                     )
-                y = y_win[s % Y_TILES]
+                y = y_win[(2 * t + b) % Y_TILES]
                 nc.scalar.copy(out=y[:, :PAIRS], in_=acc[:])
+                result = big.tile([P, S], F32, name="result", tag="big")
                 cuts = [0, 512, 768, S] if s == last else [0, S]
                 for j0, j1 in zip(cuts, cuts[1:]):
                     js = slice(j0, j1)
                     nc.vector.tensor_tensor(
-                        work[s][:, 1, js], y[:].indirect(pos3_sb[:, j0 // 16 : j1 // 16]), work[s][:, 0, js], ALU.add
+                        result[:, js], y[:].indirect(pos3_sb[:, j0 // 16 : j1 // 16]), score[s][:, js], ALU.add
                     )
-                    nc.sync.dma_start(out=out_rows[b, t][:, js], in_=work[s][:, 1, js])
+                    nc.sync.dma_start(out=out_rows[b, t][:, js], in_=result[:, js])

from contextlib import ExitStack

import concourse.mybir as mybir

F32 = mybir.dt.float32
BF16 = mybir.dt.bfloat16
I32 = mybir.dt.int32
U32 = mybir.dt.uint32
U16 = mybir.dt.uint16
U8 = mybir.dt.uint8
FP8X4 = mybir.dt.float8_e4m3fn_x4
FP4X4 = mybir.dt.float4_e2m1fn_x4
ACT = mybir.ActivationFunctionType
ALU = mybir.AluOpType

K, H, T, S, PAIRS = 1024, 1024, 2048, 1024, 512
P = 128
PACK = 4
PASS = P * PACK
BANK = 512
SLICES = H // P
Y_WINDOW = 1040
Y_TILES = 3
FLOPS = 2 * (2 * K * H * S + H * H * PAIRS)
CAST_BY = [["VS", "VS", "V", "V"], ["V", "V", "VS", "S"]]
SPLIT_QUANTIZE = [(0, 1)]


def tile_list_tissue_bubble_scores_kernel(
    tc, tab_words, tab_scales, offs, pos1, pos2, pos3, w1, w2, w4_words, w4_scales, phase, out
):
    nc = tc.nc
    with ExitStack() as ctx:
        lists = ctx.enter_context(tc.tile_pool(name="lists", bufs=1))
        keep = ctx.enter_context(tc.tile_pool(name="keep", bufs=1))
        big = ctx.enter_context(tc.tile_pool(name="big", bufs=8))
        ring3 = ctx.enter_context(tc.tile_pool(name="ring3", bufs=3))
        psum = ctx.enter_context(tc.psum_pool(name="psum", bufs=4))

        offs_sb = lists.tile([P, S // 16], U16, name="offs_sb")
        pos1_sb = lists.tile([P, PAIRS // 16], U16, name="pos1_sb")
        pos2_sb = lists.tile([P, PAIRS // 16], U16, name="pos2_sb")
        pos3_sb = lists.tile([P, S // 16], U16, name="pos3_sb")

        tab_sc = keep.tile([P, T], U8, name="tab_sc")
        nc.gpsimd.memset(tab_sc[:].bitcast(I32), 0)
        w4_sc = keep.tile([P, 2, H], U8, name="w4_sc")
        nc.gpsimd.memset(w4_sc[:].bitcast(I32), 0)
        y_win = [keep.tile([P, Y_WINDOW], F32, name="y_win%d" % i) for i in range(Y_TILES)]
        for y in y_win:
            nc.gpsimd.memset(y[:, PAIRS:], 0.0)

        nc.sync.dma_start(offs_sb[:], offs)
        tab = [keep.tile([P, T], I32, name="tab%d" % a) for a in range(2)]

        def load_tab(a):
            nc.sync.dma_start(out=tab[a][:], in_=tab_words[a].rearrange("p t i -> p (t i)").bitcast(I32))

        raw = {}

        def load_w(b, c):
            w = (w2, w1)[c // 2]
            a = c % 2
            raw[b, c] = big.tile([P, PACK, PASS], F32, name="big", tag="big")
            nc.sync.dma_start(
                out=raw[b, c][:],
                in_=w[a * PASS : (a + 1) * PASS, b * PASS : (b + 1) * PASS].rearrange("(p j) c -> p j c", j=PACK),
            )

        def load_tab_scales():
            for q in range(4):
                nc.sync.dma_start(
                    out=tab_sc[32 * q : 32 * q + 8, :].bitcast(I32),
                    in_=tab_scales[:, 4 * q : 4 * q + 4, :].bitcast(I32),
                )

        w4_raw = keep.tile([P, 2, 2 * H // 4], I32, name="w4_raw")

        def load_w4():
            for q in range(4):
                nc.sync.dma_start(
                    out=w4_sc[32 * q : 32 * q + 4, :, :].bitcast(I32),
                    in_=w4_scales[:, 4 * q : 4 * q + 4, :].rearrange("a r n -> r a n").bitcast(I32),
                )
            nc.sync.dma_start(out=w4_raw[:], in_=w4_words.rearrange("a p c -> p a c").bitcast(I32))

        phase_sb = keep.tile([P, 2, PACK], F32, name="phase_sb")
        nc.sync.dma_start(pos1_sb[:], pos1)
        nc.sync.dma_start(pos2_sb[:], pos2)
        load_tab_scales()
        load_tab(0)
        load_tab(1)
        load_w(0, 0)
        load_w(0, 1)
        load_w(0, 2)
        load_w(0, 3)
        for c in range(4):
            load_w(1, c)
        load_w4()
        nc.sync.dma_start(pos3_sb[:], pos3)
        nc.sync.dma_start(out=phase_sb[:], in_=phase.rearrange("(b p t) -> p b t", b=2, t=PACK))

        warm = keep.tile([P, 2], F32, name="warm")
        nc.gpsimd.memset(warm[:], 1.0)
        nc.scalar.activation(out=warm[:, 1:2], in_=warm[:, 0:1], func=ACT.Abs_reciprocal_sqrt)

        v_words = [keep.tile([P, S], U32, name="v_words%d" % a, align_bytes=64) for a in range(2)]
        v_sc = keep.tile([P, S], U8, name="v_sc", align_bytes=64)

        def gather_tab(a):
            nc.vector.tensor_copy(v_words[a][:], tab[a][:].bitcast(U32).indirect(offs_sb[:]))

        codes = {}
        scales = {}

        def quantize_w(b, c):
            grouped = ring3.tile([P, PACK, P, PACK], BF16, name="grouped", tag="grouped", align_bytes=64)
            dst = grouped[:].rearrange("p (u v) m j -> p m u j v", v=2)
            src = raw[b, c][:].rearrange("p j (m u v) -> p m u j v", u=2, v=2)
            engines = CAST_BY[b][c]
            for i, engine in enumerate(engines):
                copy = nc.vector.tensor_copy if engine == "V" else nc.scalar.copy
                if len(engines) == 1:
                    copy(out=dst, in_=src)
                else:
                    copy(out=dst[:, :, i], in_=src[:, :, i])
            codes[b, c] = keep.tile([P, PASS], U32, name="codes%d%d" % (b, c), align_bytes=64)
            scales[b, c] = keep.tile([P, PASS], U8, name="scales%d%d" % (b, c), align_bytes=64)
            width = PASS // 2 if (b, c) in SPLIT_QUANTIZE else PASS
            for c0 in range(0, PASS, width):
                nc.vector.quantize_mx(
                    out=codes[b, c][:, c0 : c0 + width].bitcast(FP8X4),
                    scales=scales[b, c][:, c0 : c0 + width],
                    in_=grouped[:].rearrange("p t m j -> p (t m j)")[:, PACK * c0 : PACK * (c0 + width)],
                )

        def first_product(acc, b, which, t, half):
            cols = slice(t * P, (t + 1) * P)
            js = slice(half * BANK, (half + 1) * BANK)
            for a in range(2):
                c = 2 * which + a
                nc.tensor.matmul_mx(
                    out=acc[:],
                    lhsT=codes[b, c][:, cols].bitcast(FP8X4),
                    lhsT_scale=scales[b, c][:, cols],
                    rhs=v_words[a][:, js].bitcast(FP8X4),
                    rhs_scale=v_sc[4 * a :, js],
                    start=(a == 0),
                    stop=(a == 1),
                )

        root = {}
        recip = {}

        def denominators(s):
            b, t = divmod(s, PACK)
            root[s] = ring3.tile([P, S], F32, name="root", tag="root", align_bytes=64, bufs=4)
            for half in range(2):
                acc = psum.tile([P, BANK], F32, name="load", tag="load")
                first_product(acc, b, 0, t, half)
                nc.scalar.activation(out=root[s][:, half * BANK : (half + 1) * BANK], in_=acc[:], func=ACT.Abs)
            nc.scalar.activation(out=root[s][:], in_=root[s][:], func=ACT.Abs_reciprocal_sqrt, bias=1.0)
            recip[s] = ring3.tile([P, S], F32, name="recip", tag="recip")
            nc.scalar.activation(out=recip[s][:], in_=root[s][:], func=ACT.Square)

        h = [keep.tile([P, S], F32, name="h%d" % s) for s in range(SLICES)]
        pair = [keep.tile([P, PACK, PAIRS], F32, name="pair%d" % b, align_bytes=64) for b in range(2)]

        def features(s, half):
            b, t = divmod(s, PACK)
            js = slice(half * BANK, (half + 1) * BANK)
            acc = psum.tile([P, BANK], F32, name="drive", tag="drive%d" % half, bufs=2)
            first_product(acc, b, 1, t, half)
            nc.vector.tensor_tensor(out=h[s][:, js], in0=acc[:], in1=recip[s][:, js], op=ALU.mult)

        def first_stop(s, held, m0, m1):
            nc.vector.tensor_copy(held[:, m0:m1], h[s][:].indirect(pos1_sb[:, m0 // 16 : m1 // 16]))

        def second_stop(s, held, m0, m1):
            b, t = divmod(s, PACK)
            nc.vector.tensor_tensor(
                pair[b][:, t, m0:m1], h[s][:].indirect(pos2_sb[:, m0 // 16 : m1 // 16]), held[:, m0:m1], ALU.add
            )

        pair_codes = [keep.tile([P, PAIRS], U32, name="pair_codes%d" % b, align_bytes=64) for b in range(2)]
        pair_scales = [keep.tile([P, PAIRS], U8, name="pair_scales%d" % b, align_bytes=64) for b in range(2)]

        def interleave_pair(b, grouped, copy, m0, m1):
            copy(
                out=grouped[:, PACK * m0 : PACK * m1].rearrange("p (c i t) -> p c t i", i=4, t=PACK),
                in_=pair[b][:, :, m0:m1].rearrange("p t (c i) -> p c t i", i=4),
            )

        def quantize_pair(b, grouped, m0, m1):
            nc.vector.quantize_mx(
                out=pair_codes[b][:, m0:m1].bitcast(FP8X4),
                scales=pair_scales[b][:, m0:m1],
                in_=grouped[:, PACK * m0 : PACK * m1],
            )

        w4_dealt = {}
        w4_sc_dealt = {}

        def deal_w4(t0, t1, words_tag, scales_tag):
            words = keep.tile([P, 4, t1 - t0, 2 * P], U8, name="w4_dealt%d" % t0, tag=words_tag, align_bytes=64)
            planes = keep.tile([P, 4, t1 - t0, P], U8, name="w4_sc_dealt%d" % t0, tag=scales_tag, align_bytes=64)
            nc.vector.tensor_copy(
                out=words[:].bitcast(U16),
                in_=w4_raw[:].bitcast(U16).rearrange("p a (b q t) -> p (a b) t q", b=2, t=PACK)[:, :, t0:t1, :],
            )
            nc.vector.tensor_copy(
                out=planes[:],
                in_=w4_sc[:].rearrange("p a (b q t) -> p (a b) t q", b=2, t=PACK)[:, :, t0:t1, :],
            )
            for t in range(t0, t1):
                w4_dealt[t] = words[:, :, t - t0, :]
                w4_sc_dealt[t] = planes[:, :, t - t0, :]

        nc.vector.tensor_copy(v_sc[:], tab_sc[:].indirect(offs_sb[:]))
        gather_tab(0)
        gather_tab(1)
        for c in range(4):
            quantize_w(0, c)

        last = SLICES - 1
        denominators(0)
        features(0, 0)
        features(0, 1)
        for s in range(last - 1):
            if s < PACK:
                quantize_w(1, s)
            denominators(s + 1)
            features(s + 1, 0)
            first_stop(s, root[s + 1], 0, PAIRS)
            features(s + 1, 1)
            second_stop(s, root[s + 1], 0, PAIRS)
        deal_w4(0, 1, "w4_dealt0", "w4_sc_dealt0")
        denominators(last)
        features(last, 0)
        features(last, 1)
        held = [recip[last][:, :PAIRS], recip[last][:, PAIRS:]]
        for i in range(2):
            first_stop(last - 1 + i, held[i], 0, PAIRS)
        for i in range(2):
            second_stop(last - 1 + i, held[i], 0, PAIRS)

        grouped0 = root[last][:].bitcast(BF16)
        interleave_pair(0, grouped0, nc.scalar.copy, 0, PAIRS)
        quantize_pair(0, grouped0, 0, PAIRS)
        grouped1 = keep.tile([P, PACK * PAIRS], BF16, name="grouped1", align_bytes=64)
        halves = [(0, PAIRS // 2), (PAIRS // 2, PAIRS)]

        neg_phase = pair[0][:, 0, :SLICES]
        nc.scalar.activation(
            out=neg_phase, in_=phase_sb[:].rearrange("p b t -> p (b t)"), func=ACT.Copy, scale=-1.0
        )

        score = {}

        def phase_score(s):
            score[s] = ring3.tile([P, S], F32, name="score", tag="recip")
            nc.scalar.activation(out=score[s][:], in_=h[s][:], func=ACT.Sin, scale=neg_phase[:, s : s + 1])

        phase_score(0)
        phase_score(PACK)
        interleave_pair(1, grouped1, nc.vector.tensor_copy, *halves[0])
        interleave_pair(1, grouped1, nc.scalar.copy, *halves[1])
        for m0, m1 in halves:
            quantize_pair(1, grouped1, m0, m1)
        deal_w4(1, PACK, "pair1", "grouped1")
        out_rows = out.rearrange("(b p t) j -> b t p j", b=2, t=PACK)
        for t in range(PACK):
            for b in range(2):
                s = b * PACK + t
                if t > 0:
                    phase_score(s)
                acc = psum.tile([P, BANK], F32, name="y", tag="drive0", bufs=2)
                for a in range(2):
                    nc.tensor.matmul_mx(
                        out=acc[:],
                        lhsT=w4_dealt[t][:, 2 * a + b, :].bitcast(FP4X4),
                        lhsT_scale=w4_sc_dealt[t][:, 2 * a + b, :],
                        rhs=pair_codes[a][:].bitcast(FP8X4),
                        rhs_scale=pair_scales[a][:],
                        start=(a == 0),
                        stop=(a == 1),
                    )
                y = y_win[(2 * t + b) % Y_TILES]
                nc.scalar.copy(out=y[:, :PAIRS], in_=acc[:])
                result = big.tile([P, S], F32, name="result", tag="big")
                cuts = [0, 512, 768, S] if s == last else [0, S]
                for j0, j1 in zip(cuts, cuts[1:]):
                    js = slice(j0, j1)
                    nc.vector.tensor_tensor(
                        result[:, js], y[:].indirect(pos3_sb[:, j0 // 16 : j1 // 16]), score[s][:, js], ALU.add
                    )
                    nc.sync.dma_start(out=out_rows[b, t][:, js], in_=result[:, js])
